import numpy as np, ml_dtypes
CORES = [1,17,65,89,97,113]
N = 6
TK = 128
COEF = [[3,1,1,1,1,1],[1,3,1,1,1,1],[1,1,3,1,1,1],[1,1,1,3,1,1],[1,1,1,1,3,1],[1,1,1,1,1,3]]
def setup_inputs(rng):
    return {"x": rng.standard_normal((N, 128, TK), dtype=np.float32).astype(ml_dtypes.bfloat16), "a": (rng.standard_normal((N, 128, 128), dtype=np.float32) / 11).astype(ml_dtypes.bfloat16)}
def setup_inputs_big(rng):
    d = setup_inputs(rng)
    for k in ("x", "a"): d[k] = (d[k].astype(np.float32) * 1024.0).astype(d[k].dtype)
    return d
def setup_inputs_small(rng):
    d = setup_inputs(rng)
    for k in ("x", "a"): d[k] = (d[k].astype(np.float32) * (1 / 1024.0)).astype(d[k].dtype)
    return d
def setup_inputs_apart(rng):
    d = setup_inputs(rng)
    f = (10.0 ** rng.permutation(np.linspace(-1.5, 1.5, N))).astype(np.float32).reshape(N, 1, 1)
    for k in ("x", "a"): d[k] = (d[k].astype(np.float32) * f).astype(d[k].dtype)
    return d
def reference(x, a):
    X, A = x.astype(np.float64), a.astype(np.float64)
    y = np.stack([A[r].T @ sum(COEF[r][j] * X[j] for j in range(N)) for r in range(N)])
    return {"y": y.astype(ml_dtypes.bfloat16)}

from concourse.bass import DstId, RemoteDMATransfer

_N = 6
SCRATCH = {
    "xs": ("dram", [128, 128], "bfloat16"),
    "xo": ("sbuf", [128, 128], "bfloat16"),
    "aa": ("sbuf", [128, 128], "bfloat16"),
    "yo": ("sbuf", [128, 128], "bfloat16"),
    "acc": ("psum", [128, 128], "float32"),
}
for _j in range(_N):
    SCRATCH["land%d" % _j] = ("sbuf", [128, 128], "bfloat16")

SEMAPHORES = ["staged", "a_in", "x_in", "handed", "sent", "summed", "rounded", "stored"] + ["arr%d" % _j for _j in range(_N)]

LONG_ONE = 4
LONG_MANY = 8
SHORT = 8


def _engines(allowed, n):
    bits = [b for b in range(allowed.bit_length()) if (allowed >> b) & 1]
    step = max(1, len(bits) // n)
    m = 0
    for b in bits[::step][:n]:
        m |= 1 << b
    return m


def _plan(T, topo):
    cores = list(T.cores)
    n = len(cores)
    coef = T.tables["COEF"]
    spare = [c for c in range(topo.CHIPS * topo.CORES_PER_CHIP) if c not in cores]
    direct, forced, cands = {}, {}, {}
    for j in range(n):
        want = [(j + 1 + k) % n for k in range(n - 1)]
        want = [r for r in want if coef[r][j]]
        direct[j] = [r for r in want if topo.may_write(cores[j], cores[r])]
        forced[j] = [r for r in want if r not in direct[j]]
        cands[j] = [h for h in spare if topo.chip(h) == topo.chip(cores[j])]
    cap = 0
    for j in range(n):
        if forced[j]:
            hs = [h for h in cands[j] if all(topo.may_write(h, cores[r]) for r in forced[j])]
            cap = max(cap, -(-len(forced[j]) // len(hs)))
    late = {}
    relay = {j: {} for j in range(n)}
    taken = {}
    for j in sorted(range(n), key=lambda q: len(forced[q])):
        for r in forced[j]:
            ok = [h for h in cands[j]
                  if topo.may_write(h, cores[r]) and taken.get(h, j) == j and len(relay[j].get(h, [])) < cap]
            h = min(ok, key=lambda q: (late.get((topo.chip(cores[r]), topo.die(q)), 0), len(relay[j].get(q, [])),
                                       topo.die(q) != topo.die(cores[j]), q))
            taken[h] = j
            relay[j].setdefault(h, []).append(r)
            k = (topo.chip(cores[r]), topo.die(h))
            late[k] = late.get(k, 0) + 1
        for h in list(relay[j]):
            while len(relay[j][h]) < cap and len(direct[j]) > len(relay[j][h]):
                r = direct[j].pop()
                relay[j][h].append(r)
                k = (topo.chip(cores[r]), topo.die(h))
                late[k] = late.get(k, 0) + 1
    return direct, relay


def _handovers(relay_j):
    hs = sorted(relay_j, key=lambda h: (-len(relay_j[h]), h))
    if not hs:
        return []
    top = len(relay_j[hs[0]])
    first = [h for h in hs if len(relay_j[h]) == top]
    rest = [h for h in hs if len(relay_j[h]) < top]
    return [grp for grp in (first, rest) if grp]


def _send(g, T, topo, dests, src, dst, sem, mask):
    where = [topo.addr(d) for d in dests]
    if len(dests) == 1:
        g.remote_dma(out_ap=dst, in_ap=src, remote_sem=sem, local_sem=T.sem.sent, pid=where[0][1],
                     routing_id=where[0][0], dma_engine_mask=mask)
    else:
        g.remote_dma_fused([RemoteDMATransfer(dst_ids=[DstId(rid=w[0], pnc=w[1]) for w in where], dma_engine_mask=mask,
                                              remote_sem=sem, srcs=[src], dsts=[dst] * len(dests), alu_op=0)],
                           local_sem=T.sem.sent)
    return bin(mask).count("1")


def rank_program(g, core, T, topo):
    cores = list(T.cores)
    n = len(cores)
    coef = T.tables["COEF"]
    direct, relay = _plan(T, topo)
    rank = T.rank_of(core)

    if rank is None:
        for j in range(n):
            if core in relay[j]:
                for grp in _handovers(relay[j]):
                    if core in grp:
                        g.wait_ge(T.sem.handed, LONG_ONE if len(grp) == 1 else LONG_MANY)
                dests = [cores[r] for r in relay[j][core]]
                allowed = topo.mask(core, dests[0])
                for d in dests:
                    allowed &= topo.mask(core, d)
                out = _send(g, T, topo, dests, T.xs[:], T["land%d" % j][:], T.sem["arr%d" % j], _engines(allowed, SHORT))
                g.wait_ge(T.sem.sent, out)
        return

    g.sync.dma_start(T.xs[:], T.x[:]).then_inc(T.sem.staged, 16)
    g.scalar.dma_start(T.aa[:], T.a[:]).then_inc(T.sem.a_in, 16)
    g.scalar.dma_start(T.xo[:], T.x[:]).then_inc(T.sem.x_in, 16)

    allowed = None
    for d in list(relay[rank]) + [cores[r] for r in direct[rank]]:
        allowed = topo.mask(core, d) if allowed is None else allowed & topo.mask(core, d)
    out = 0
    g.wait_ge(T.sem.staged, 16)
    for grp in _handovers(relay[rank]):
        out += _send(g, T, topo, grp, T.xs[:], T.xs[:], T.sem.handed,
                     _engines(allowed, LONG_ONE if len(grp) == 1 else LONG_MANY))
    if direct[rank]:
        out += _send(g, T, topo, [cores[r] for r in direct[rank]], T.xs[:], T["land%d" % rank][:],
                     T.sem["arr%d" % rank], _engines(allowed, SHORT))

    expect = []
    for j in range(n):
        if j == rank or not coef[rank][j]:
            continue
        if rank in direct[j]:
            expect.append((0, 0, direct[j].index(rank), j))
        else:
            calls = _handovers(relay[j])
            for h in relay[j]:
                if rank in relay[j][h]:
                    call = [i for i in range(len(calls)) if h in calls[i]][0]
                    expect.append((1, relay[j][h].index(rank), call, j))
    steps = [(None, T.xo)] * coef[rank][rank]
    for e in sorted(expect):
        j = e[3]
        steps += [(T.sem["arr%d" % j], T["land%d" % j])] + [(None, T["land%d" % j])] * (coef[rank][j] - 1)
    te = g.tensor
    te.wait_ge(T.sem.a_in, 16)
    te.wait_ge(T.sem.x_in, 16)
    for i in range(len(steps)):
        sem, buf = steps[i]
        if sem is not None:
            te.wait_ge(sem, SHORT)
        mm = te.matmul(T.acc[:], T.aa[:], buf[:], start=(i == 0), stop=(i == len(steps) - 1))
        if i == len(steps) - 1:
            mm.then_inc(T.sem.summed, 1)

    g.vector.wait_ge(T.sem.summed, 1)
    g.vector.tensor_copy(T.yo[:], T.acc[:]).then_inc(T.sem.rounded, 1)
    g.sync.wait_ge(T.sem.rounded, 1)
    g.sync.dma_start(T.y[:], T.yo[:]).then_inc(T.sem.stored, 16)
    g.sync.wait_ge(T.sem.stored, 16)
    if out:
        g.wait_ge(T.sem.sent, out)
